import numpy as np
import ml_dtypes


def mxq(x, axis, fmt="e4m3"):
    dtype, down = {"e4m3": (ml_dtypes.float8_e4m3fn, 7), "e5m2": (ml_dtypes.float8_e5m2, 14)}[fmt]
    v = np.moveaxis(np.asarray(x, np.float32).astype(ml_dtypes.bfloat16).astype(np.float64), axis, -1)
    blocks = v.reshape(v.shape[:-1] + (-1, 32))
    amax = np.abs(blocks).max(-1, keepdims=True)
    byte = np.maximum(np.where(amax > 0, np.frexp(amax)[1] - 1 + 127, 0) - down, 1)
    scale = np.exp2(byte - 127.0)
    codes = (blocks / scale).astype(np.float32).astype(dtype).astype(np.float64)
    return np.moveaxis((codes * scale).reshape(v.shape), -1, axis)


WIDE = False


def mx_kscale(k):
    if not WIDE:
        return np.ones(k)
    levels = np.array([30, -30])
    if k % 512:
        return np.exp2(np.random.permutation(np.resize(levels, k // 32))).repeat(32)
    a = np.empty((k // 512, 16))
    for p in range(k // 512):
        a[p, :8] = np.random.permutation(np.resize(levels, 8))
        for g in range(8):
            far = levels[np.abs(levels - a[p, g]) >= 10]
            a[p, g + 8] = far[np.random.randint(len(far))]
    return np.exp2(a.ravel()).repeat(32)


def f64(x):
    return np.asarray(x).astype(np.float64)


def striped(idx):
    return np.tile(np.asarray(idx).reshape(-1, 16).T, (8, 1)).astype(np.uint16)


def unstriped(offs):
    return offs[:16].T.reshape(-1).astype(np.int64)


E2M1 = np.array([0.0, 0.5, 1.0, 1.5, 2.0, 3.0, 4.0, 6.0, -0.0, -0.5, -1.0, -1.5, -2.0, -3.0, -4.0, -6.0])


def pack_weight(w, fmt):
    k, n = w.shape
    w = f64(np.asarray(w, np.float32).astype(ml_dtypes.bfloat16)).reshape(k // 32, 32, n)
    amax = np.abs(w).max(1)
    if fmt == "e4m3":
        byte = np.frexp(amax)[1] - 1 + 127 - 7
    else:
        mant, ex = np.frexp(amax / 6.0)
        byte = np.where(mant > 0.5, ex, ex - 1) + 127
    byte = np.clip(np.where(amax > 0, byte, 1), 1, 254)
    scaled = (w * np.exp2(127.0 - byte)[:, None, :]).reshape(k, n).astype(np.float32)
    by_word = np.ascontiguousarray(scaled.reshape(k // 512, 128, 4, n).transpose(0, 1, 3, 2))
    if fmt == "e4m3":
        words = by_word.astype(ml_dtypes.float8_e4m3fn).view(np.uint8)
    else:
        c = by_word.astype(ml_dtypes.float4_e2m1fn).view(np.uint8) & 0xF
        words = (c[..., 0::2] | (c[..., 1::2] << 4)).reshape(k // 512, 128, 2 * n)
    return np.ascontiguousarray(words), np.ascontiguousarray(byte.astype(np.uint8).reshape(k // 512, 16, n))


def unpack_weight(words, scales, fmt):
    g, _, n = scales.shape
    words = np.ascontiguousarray(words).reshape(g, 128, n, -1)
    if fmt == "e4m3":
        vals = words.view(ml_dtypes.float8_e4m3fn).astype(np.float64)
    else:
        nib = np.empty((g, 128, n, 4), np.uint8)
        nib[..., 0::2] = words & 0xF
        nib[..., 1::2] = words >> 4
        vals = E2M1[nib]
    vals = vals * np.repeat(np.exp2(scales.astype(np.float64) - 127.0), 8, axis=1)[..., None]
    return vals.transpose(0, 1, 3, 2).reshape(g * 512, n)


def sigmoid(v):
    return 1.0 / (1.0 + np.exp(-v))


K, T, J, R, C, N, E = 512, 2048, 256, 512, 512, 256, 1024


def setup_inputs():
    n = np.random.standard_normal
    idx = np.random.permutation(T)[:J]
    idx2 = np.random.permutation(T)[:J]
    idx3 = np.random.permutation(C)[:J]
    idx4 = np.random.permutation(C)[:J]
    idx5 = np.random.permutation(E)[:J]
    fk = mx_kscale(K)
    fr = mx_kscale(R)
    xtp = pack_weight(n((K, T)) / fk[:, None], "e2m1")
    wp = pack_weight(n((K, R)) * 1 / np.sqrt(K) * fk[:, None] * fr, "e4m3")
    wbp = pack_weight(n((R, N)) * 1 / np.sqrt(R) / fr[:, None], "e2m1")
    return {
        "xt_words": xtp[0],
        "xt_scales": xtp[1],
        "w_words": wp[0],
        "w_scales": wp[1],
        "wb_words": wbp[0],
        "wb_scales": wbp[1],
        "tz": (n((N, E))).astype(np.float32),
        "so": (np.random.uniform(0.6, 1.6, (N, 1))).astype(np.float32),
        "bo": (np.random.uniform(-1.0, 1.0, (N, 1))).astype(np.float32),
        "offs": striped(idx),
        "offs2": striped(idx2),
        "offs3": striped(idx3),
        "offs4": striped(idx4),
        "offs5": striped(idx5),
    }


def reference(xt_words, xt_scales, w_words, w_scales, wb_words, wb_scales, tz, so, bo, offs, offs2, offs3, offs4, offs5):
    idx = unstriped(offs)
    idx2 = unstriped(offs2)
    idx3 = unstriped(offs3)
    idx4 = unstriped(offs4)
    idx5 = unstriped(offs5)
    xtu = unpack_weight(xt_words, xt_scales, "e2m1")
    wu = unpack_weight(w_words, w_scales, "e4m3")
    wbu = unpack_weight(wb_words, wb_scales, "e2m1")
    xtidxg = xtu[:, idx]
    a = wu.T @ xtidxg
    xtidx2g = xtu[:, idx2]
    b = wu.T @ xtidx2g
    pw = np.zeros((R, C))
    pw[:, idx3] = a
    hid = np.abs(pw[:, idx4] - b)
    hidq = mxq(hid, 0, "e5m2")
    p = wbu.T @ hidq
    y = p * sigmoid(f64(tz)[:, idx5] * f64(so) + f64(bo))
    return y

@@ -1,0 +1,170 @@
+from contextlib import ExitStack
+
+import concourse.mybir as mybir
+
+K, T, J, R, C, N, E = 512, 2048, 256, 512, 512, 256, 1024
+FLOPS = 2 * K * R * J * 2 + 2 * R * N * J
+
+F32 = mybir.dt.float32
+BF16 = mybir.dt.bfloat16
+I32 = mybir.dt.int32
+U32 = mybir.dt.uint32
+U16 = mybir.dt.uint16
+U8 = mybir.dt.uint8
+E4M3X4 = mybir.dt.float8_e4m3fn_x4
+E5M2X4 = mybir.dt.float8_e5m2_x4
+E2M1X4 = mybir.dt.float4_e2m1fn_x4
+ACT = mybir.ActivationFunctionType
+ALU = mybir.AluOpType
+
+P = 128
+PACK = 4
+QUADS = 4
+
+
+def load_scale_rows(queue, plane, rows):
+    for q in range(QUADS):
+        queue.dma_start(plane[32 * q : 32 * q + 4, :].bitcast(I32), rows[4 * q : 4 * q + 4, :].bitcast(I32))
+
+
+def tile_list_tied_board_one_finalgate_kernel(
+    tc, xt_words, xt_scales, w_words, w_scales, wb_words, wb_scales, tz, so, bo, offs, offs2, offs3, offs4, offs5, out
+):
+    nc = tc.nc
+    with ExitStack() as ctx:
+        lists = ctx.enter_context(tc.tile_pool(name="lists", bufs=1))
+        keep = ctx.enter_context(tc.tile_pool(name="keep", bufs=1))
+        psum = ctx.enter_context(tc.psum_pool(name="psum", bufs=1))
+
+        first, second, put, read, entry = [lists.tile([P, J // 16], U16, name=f"list{i}") for i in range(5)]
+
+        xw = keep.tile([P, T], U16, align_bytes=64)
+        xs = keep.tile([P, T], U8, align_bytes=64)
+        ww = keep.tile([P, R], U32, align_bytes=64)
+        ws = keep.tile([P, R], U8, align_bytes=64)
+        wbw = keep.tile([P, 2 * N], U8, align_bytes=64)
+        wbs = keep.tile([P, N], U8, align_bytes=64)
+        boards = [keep.tile([P, C], F32, name=f"board{t}", align_bytes=64) for t in range(PACK)]
+        tzs = [keep.tile([P, E], F32, name=f"tz{h}", align_bytes=64) for h in range(2)]
+        slope = keep.tile([P, 2], F32)
+        offset = keep.tile([P, 2], F32)
+
+        nc.vector.memset(xs[:, : T // 2].bitcast(I32), 0)
+        nc.gpsimd.memset(xs[:, T // 2 :].bitcast(I32), 0)
+        nc.vector.memset(ws[:].bitcast(I32), 0)
+        nc.vector.memset(wbs[:].bitcast(I32), 0)
+        for t in range(PACK):
+            nc.vector.memset(boards[t][:], 0.0)
+
+        warm_in = keep.tile([P, 1], F32)
+        warm_out = keep.tile([P, 1], F32)
+        nc.gpsimd.memset(warm_in[:], 0.0)
+        nc.scalar.activation(warm_out[:], warm_in[:], ACT.Sigmoid)
+
+        nc.sync.dma_start(first[:], offs)
+        nc.sync.dma_start(second[:], offs2)
+        nc.sync.dma_start(ww[:].bitcast(I32), w_words[0].rearrange("p n t -> p (n t)").bitcast(I32))
+        load_scale_rows(nc.sync, xs, xt_scales[0])
+        nc.sync.dma_start(xw[:].bitcast(I32), xt_words[0].bitcast(I32))
+        load_scale_rows(nc.sync, ws, w_scales[0])
+        nc.sync.dma_start(put[:], offs3)
+        nc.sync.dma_start(read[:], offs4)
+        for h in range(2):
+            nc.sync.dma_start(tzs[h][:], tz[h * P : (h + 1) * P, :])
+        nc.sync.dma_start(wbw[:].bitcast(I32), wb_words[0].bitcast(I32))
+        load_scale_rows(nc.sync, wbs, wb_scales[0])
+        nc.sync.dma_start(entry[:], offs5)
+        with nc.allow_non_contiguous_dma(reason="one value a partition"):
+            nc.sync.dma_start(slope[:], so.rearrange("(h p) o -> p (h o)", p=P))
+            nc.sync.dma_start(offset[:], bo.rearrange("(h p) o -> p (h o)", p=P))
+
+        xa_w = keep.tile([P, J], U16, align_bytes=64)
+        xa_s = keep.tile([P, J], U8, align_bytes=64)
+        xb_w = keep.tile([P, J], U16, align_bytes=64)
+        xb_s = keep.tile([P, J], U8, align_bytes=64)
+        wp = keep.tile([P, R], U32, align_bytes=64)
+        wsp = [keep.tile([P, P], U8, name=f"wsp{t}", align_bytes=64) for t in range(PACK)]
+
+        nc.vector.tensor_copy(
+            wp[:].rearrange("p (t m i) -> p m t i", t=PACK, i=4), ww[:].rearrange("p (m i t) -> p m t i", t=PACK, i=4)
+        )
+        nc.vector.tensor_copy(xa_s[:], xs[:].indirect(first[:]))
+        nc.vector.tensor_copy(xb_s[:], xs[:].indirect(second[:]))
+        nc.vector.tensor_copy(xa_w[:], xw[:].indirect(first[:]))
+        for t in (0, 2, 1, 3):
+            nc.gpsimd.tensor_copy(wsp[t][:], ws[:].rearrange("p (m t) -> p t m", t=PACK)[:, t, :])
+
+        def first_stage(dst, t, words, scales):
+            cols = slice(t * P, (t + 1) * P)
+            nc.tensor.matmul_mx(
+                out=dst,
+                lhsT=wp[:, cols].bitcast(E4M3X4),
+                lhsT_scale=wsp[t][:],
+                rhs=words[:].bitcast(E2M1X4),
+                rhs_scale=scales[:],
+                start=True,
+                stop=True,
+            )
+
+        a_ps = [psum.tile([P, J], F32, name=f"a_ps{t}") for t in range(PACK)]
+        for t in (0, 2, 1, 3):
+            first_stage(a_ps[t][:], t, xa_w, xa_s)
+
+        nc.vector.tensor_copy(xb_w[:], xw[:].indirect(second[:]))
+        b_ps = [psum.tile([P, 2, J], F32, name=f"b_ps{u}") for u in range(2)]
+        for t in range(PACK):
+            first_stage(b_ps[t // 2][:, t % 2, :], t, xb_w, xb_s)
+
+        a_sb = [keep.tile([P, J], F32, name=f"a_sb{t}", align_bytes=64) for t in range(PACK)]
+        picked = [keep.tile([P, J], F32, name=f"picked{t}", align_bytes=64) for t in range(PACK)]
+        diff = keep.tile([P, PACK, J], F32, name="diff", tag="diff_then_gate", align_bytes=64)
+
+        def pick_on_scalar(t):
+            nc.scalar.activation(picked[t][:], boards[t][:].indirect(read[:]), ACT.Copy)
+
+        def subtract(t):
+            nc.vector.tensor_tensor(diff[:, t, :], picked[t][:], b_ps[t // 2][:, t % 2, :], ALU.subtract)
+
+        nc.scalar.copy(a_sb[0][:], a_ps[0][:])
+        nc.scalar.activation(boards[0][:].indirect(put[:]), a_sb[0][:], ACT.Copy)
+        for t in (2, 3):
+            nc.vector.tensor_copy(a_sb[t][:], a_ps[t][:])
+            nc.vector.tensor_copy(boards[t][:].indirect(put[:]), a_sb[t][:])
+        nc.scalar.copy(a_sb[1][:], a_ps[1][:])
+        pick_on_scalar(0)
+        nc.scalar.activation(boards[1][:].indirect(put[:]), a_sb[1][:], ACT.Copy)
+        pick_on_scalar(2)
+        pick_on_scalar(1)
+        subtract(0)
+        nc.vector.tensor_copy(picked[3][:], boards[3][:].indirect(read[:]))
+        for t in (2, 3, 1):
+            subtract(t)
+
+        hid = keep.tile([P, J, PACK], BF16, align_bytes=64)
+        half = J // 2
+        woven = diff[:].rearrange("p t j -> p j t")
+        nc.scalar.activation(hid[:, :half, :], woven[:, :half, :], ACT.Abs)
+        nc.vector.scalar_tensor_tensor(hid[:, half:, :], woven[:, half:, :], -1.0, woven[:, half:, :], ALU.mult, ALU.max)
+
+        codes = keep.tile([P, J], U32, align_bytes=64)
+        scales = keep.tile([P, J], U8, align_bytes=64)
+        nc.vector.quantize_mx(out=codes[:].bitcast(E5M2X4), scales=scales[:], in_=hid[:].rearrange("p j t -> p (j t)"))
+
+        gate = keep.tile([P, PACK, J], F32, name="gate", tag="diff_then_gate", align_bytes=64)
+        res = [keep.tile([P, J], F32, name=f"res{h}", align_bytes=64) for h in range(2)]
+        for h in range(2):
+            nc.scalar.activation(
+                gate[:, h, :], tzs[h][:].indirect(entry[:]), ACT.Sigmoid, bias=offset[:, h : h + 1], scale=slope[:, h : h + 1]
+            )
+            p_ps = psum.tile([P, J], F32, name=f"p_ps{h}")
+            nc.tensor.matmul_mx(
+                out=p_ps[:],
+                lhsT=wbw[:, 2 * P * h : 2 * P * (h + 1)].bitcast(E2M1X4),
+                lhsT_scale=wbs[:, P * h : P * (h + 1)],
+                rhs=codes[:].bitcast(E5M2X4),
+                rhs_scale=scales[:],
+                start=True,
+                stop=True,
+            )
+            nc.vector.tensor_tensor(res[h][:], gate[:, h, :], p_ps[:], ALU.mult)
+            (nc.sync if h == 0 else nc.scalar).dma_start(out[h * P : (h + 1) * P, :], res[h][:])

@@ -38,14 +38,13 @@ def tile_list_tied_board_one_finalgate_kernel(
 
         first, second, put, read, entry = [lists.tile([P, J // 16], U16, name=f"list{i}") for i in range(5)]
 
-        xw = keep.tile([P, T], U16, align_bytes=64)
-        xs = keep.tile([P, T], U8, align_bytes=64)
+        xw = keep.tile([P, T], U16, tag="xw_then_tz", align_bytes=64)
+        xs = keep.tile([P, T], U8, tag="xs_then_tz", align_bytes=64)
         ww = keep.tile([P, R], U32, align_bytes=64)
-        ws = keep.tile([P, R], U8, align_bytes=64)
+        ws = keep.tile([P, R], U8, tag="ws_then_xb_w", align_bytes=64)
         wbw = keep.tile([P, 2 * N], U8, align_bytes=64)
         wbs = keep.tile([P, N], U8, align_bytes=64)
         boards = [keep.tile([P, C], F32, name=f"board{t}", align_bytes=64) for t in range(PACK)]
-        tzs = [keep.tile([P, E], F32, name=f"tz{h}", align_bytes=64) for h in range(2)]
         slope = keep.tile([P, 2], F32)
         offset = keep.tile([P, 2], F32)
 
@@ -69,8 +68,6 @@ def tile_list_tied_board_one_finalgate_kernel(
         load_scale_rows(nc.sync, ws, w_scales[0])
         nc.sync.dma_start(put[:], offs3)
         nc.sync.dma_start(read[:], offs4)
-        for h in range(2):
-            nc.sync.dma_start(tzs[h][:], tz[h * P : (h + 1) * P, :])
         nc.sync.dma_start(wbw[:].bitcast(I32), wb_words[0].bitcast(I32))
         load_scale_rows(nc.sync, wbs, wb_scales[0])
         nc.sync.dma_start(entry[:], offs5)
@@ -80,10 +77,12 @@ def tile_list_tied_board_one_finalgate_kernel(
 
         xa_w = keep.tile([P, J], U16, align_bytes=64)
         xa_s = keep.tile([P, J], U8, align_bytes=64)
-        xb_w = keep.tile([P, J], U16, align_bytes=64)
+        xb_w = keep.tile([P, J], U16, tag="ws_then_xb_w", align_bytes=64)
         xb_s = keep.tile([P, J], U8, align_bytes=64)
         wp = keep.tile([P, R], U32, align_bytes=64)
-        wsp = [keep.tile([P, P], U8, name=f"wsp{t}", align_bytes=64) for t in range(PACK)]
+        wsp_first = keep.tile([P, P], U8, align_bytes=64)
+        wsp_rest = keep.tile([P, (PACK - 1) * P], U8, align_bytes=64)
+        wsp = [wsp_first[:]] + [wsp_rest[:, t * P : (t + 1) * P] for t in range(PACK - 1)]
 
         nc.vector.tensor_copy(
             wp[:].rearrange("p (t m i) -> p m t i", t=PACK, i=4), ww[:].rearrange("p (m i t) -> p m t i", t=PACK, i=4)
@@ -91,15 +90,16 @@ def tile_list_tied_board_one_finalgate_kernel(
         nc.vector.tensor_copy(xa_s[:], xs[:].indirect(first[:]))
         nc.vector.tensor_copy(xb_s[:], xs[:].indirect(second[:]))
         nc.vector.tensor_copy(xa_w[:], xw[:].indirect(first[:]))
-        for t in (0, 2, 1, 3):
-            nc.gpsimd.tensor_copy(wsp[t][:], ws[:].rearrange("p (m t) -> p t m", t=PACK)[:, t, :])
+        dealt = ws[:].rearrange("p (m i t) -> p m t i", t=PACK, i=16)
+        nc.vector.tensor_copy(wsp_first[:].rearrange("p (m i) -> p m i", i=16), dealt[:, :, 0, :])
+        nc.vector.tensor_copy(wsp_rest[:].rearrange("p (t m i) -> p m t i", t=PACK - 1, i=16), dealt[:, :, 1:, :])
 
         def first_stage(dst, t, words, scales):
             cols = slice(t * P, (t + 1) * P)
             nc.tensor.matmul_mx(
                 out=dst,
                 lhsT=wp[:, cols].bitcast(E4M3X4),
-                lhsT_scale=wsp[t][:],
+                lhsT_scale=wsp[t],
                 rhs=words[:].bitcast(E2M1X4),
                 rhs_scale=scales[:],
                 start=True,
@@ -111,6 +111,11 @@ def tile_list_tied_board_one_finalgate_kernel(
             first_stage(a_ps[t][:], t, xa_w, xa_s)
 
         nc.vector.tensor_copy(xb_w[:], xw[:].indirect(second[:]))
+        tzs = [
+            keep.tile([P, E], F32, name=f"tz{h}", tag=tag, align_bytes=64) for h, tag in enumerate(("xs_then_tz", "xw_then_tz"))
+        ]
+        for h in range(2):
+            nc.sync.dma_start(tzs[h][:], tz[h * P : (h + 1) * P, :])
         b_ps = [psum.tile([P, 2, J], F32, name=f"b_ps{u}") for u in range(2)]
         for t in range(PACK):
             first_stage(b_ps[t // 2][:, t % 2, :], t, xb_w, xb_s)
@@ -141,9 +146,13 @@ def tile_list_tied_board_one_finalgate_kernel(
             subtract(t)
 
         hid = keep.tile([P, J, PACK], BF16, align_bytes=64)
-        half = J // 2
+        half = 160
         woven = diff[:].rearrange("p t j -> p j t")
-        nc.scalar.activation(hid[:, :half, :], woven[:, :half, :], ACT.Abs)
+        nc.scalar.activation(
+            hid[:, :half, :].rearrange("p (c i) t -> p c t i", i=4),
+            diff[:, :, :half].rearrange("p t (c i) -> p c t i", i=4),
+            ACT.Abs,
+        )
         nc.vector.scalar_tensor_tensor(hid[:, half:, :], woven[:, half:, :], -1.0, woven[:, half:, :], ALU.mult, ALU.max)
 
         codes = keep.tile([P, J], U32, align_bytes=64)

from contextlib import ExitStack

import concourse.mybir as mybir

K, T, J, R, C, N, E = 512, 2048, 256, 512, 512, 256, 1024
FLOPS = 2 * K * R * J * 2 + 2 * R * N * J

F32 = mybir.dt.float32
BF16 = mybir.dt.bfloat16
I32 = mybir.dt.int32
U32 = mybir.dt.uint32
U16 = mybir.dt.uint16
U8 = mybir.dt.uint8
E4M3X4 = mybir.dt.float8_e4m3fn_x4
E5M2X4 = mybir.dt.float8_e5m2_x4
E2M1X4 = mybir.dt.float4_e2m1fn_x4
ACT = mybir.ActivationFunctionType
ALU = mybir.AluOpType

P = 128
PACK = 4
QUADS = 4


def load_scale_rows(queue, plane, rows):
    for q in range(QUADS):
        queue.dma_start(plane[32 * q : 32 * q + 4, :].bitcast(I32), rows[4 * q : 4 * q + 4, :].bitcast(I32))


def tile_list_tied_board_one_finalgate_kernel(
    tc, xt_words, xt_scales, w_words, w_scales, wb_words, wb_scales, tz, so, bo, offs, offs2, offs3, offs4, offs5, out
):
    nc = tc.nc
    with ExitStack() as ctx:
        lists = ctx.enter_context(tc.tile_pool(name="lists", bufs=1))
        keep = ctx.enter_context(tc.tile_pool(name="keep", bufs=1))
        psum = ctx.enter_context(tc.psum_pool(name="psum", bufs=1))

        first, second, put, read, entry = [lists.tile([P, J // 16], U16, name=f"list{i}") for i in range(5)]

        xw = keep.tile([P, T], U16, tag="xw_then_tz", align_bytes=64)
        xs = keep.tile([P, T], U8, tag="xs_then_tz", align_bytes=64)
        ww = keep.tile([P, R], U32, align_bytes=64)
        ws = keep.tile([P, R], U8, tag="ws_then_xb_w", align_bytes=64)
        wbw = keep.tile([P, 2 * N], U8, align_bytes=64)
        wbs = keep.tile([P, N], U8, align_bytes=64)
        boards = [keep.tile([P, C], F32, name=f"board{t}", align_bytes=64) for t in range(PACK)]
        slope = keep.tile([P, 2], F32)
        offset = keep.tile([P, 2], F32)

        nc.vector.memset(xs[:, : T // 2].bitcast(I32), 0)
        nc.gpsimd.memset(xs[:, T // 2 :].bitcast(I32), 0)
        nc.vector.memset(ws[:].bitcast(I32), 0)
        nc.vector.memset(wbs[:].bitcast(I32), 0)
        for t in range(PACK):
            nc.vector.memset(boards[t][:], 0.0)

        warm_in = keep.tile([P, 1], F32)
        warm_out = keep.tile([P, 1], F32)
        nc.gpsimd.memset(warm_in[:], 0.0)
        nc.scalar.activation(warm_out[:], warm_in[:], ACT.Sigmoid)

        nc.sync.dma_start(first[:], offs)
        nc.sync.dma_start(second[:], offs2)
        nc.sync.dma_start(ww[:].bitcast(I32), w_words[0].rearrange("p n t -> p (n t)").bitcast(I32))
        load_scale_rows(nc.sync, xs, xt_scales[0])
        nc.sync.dma_start(xw[:].bitcast(I32), xt_words[0].bitcast(I32))
        load_scale_rows(nc.sync, ws, w_scales[0])
        nc.sync.dma_start(put[:], offs3)
        nc.sync.dma_start(read[:], offs4)
        nc.sync.dma_start(wbw[:].bitcast(I32), wb_words[0].bitcast(I32))
        load_scale_rows(nc.sync, wbs, wb_scales[0])
        nc.sync.dma_start(entry[:], offs5)
        with nc.allow_non_contiguous_dma(reason="one value a partition"):
            nc.sync.dma_start(slope[:], so.rearrange("(h p) o -> p (h o)", p=P))
            nc.sync.dma_start(offset[:], bo.rearrange("(h p) o -> p (h o)", p=P))

        xa_w = keep.tile([P, J], U16, align_bytes=64)
        xa_s = keep.tile([P, J], U8, align_bytes=64)
        xb_w = keep.tile([P, J], U16, tag="ws_then_xb_w", align_bytes=64)
        xb_s = keep.tile([P, J], U8, align_bytes=64)
        wp = keep.tile([P, R], U32, align_bytes=64)
        wsp_first = keep.tile([P, P], U8, align_bytes=64)
        wsp_rest = keep.tile([P, (PACK - 1) * P], U8, align_bytes=64)
        wsp = [wsp_first[:]] + [wsp_rest[:, t * P : (t + 1) * P] for t in range(PACK - 1)]

        nc.vector.tensor_copy(
            wp[:].rearrange("p (t m i) -> p m t i", t=PACK, i=4), ww[:].rearrange("p (m i t) -> p m t i", t=PACK, i=4)
        )
        nc.vector.tensor_copy(xa_s[:], xs[:].indirect(first[:]))
        nc.vector.tensor_copy(xb_s[:], xs[:].indirect(second[:]))
        nc.vector.tensor_copy(xa_w[:], xw[:].indirect(first[:]))
        dealt = ws[:].rearrange("p (m i t) -> p m t i", t=PACK, i=16)
        nc.vector.tensor_copy(wsp_first[:].rearrange("p (m i) -> p m i", i=16), dealt[:, :, 0, :])
        nc.vector.tensor_copy(wsp_rest[:].rearrange("p (t m i) -> p m t i", t=PACK - 1, i=16), dealt[:, :, 1:, :])

        def first_stage(dst, t, words, scales):
            cols = slice(t * P, (t + 1) * P)
            nc.tensor.matmul_mx(
                out=dst,
                lhsT=wp[:, cols].bitcast(E4M3X4),
                lhsT_scale=wsp[t],
                rhs=words[:].bitcast(E2M1X4),
                rhs_scale=scales[:],
                start=True,
                stop=True,
            )

        a_ps = [psum.tile([P, J], F32, name=f"a_ps{t}") for t in range(PACK)]
        for t in (0, 2, 1, 3):
            first_stage(a_ps[t][:], t, xa_w, xa_s)

        nc.vector.tensor_copy(xb_w[:], xw[:].indirect(second[:]))
        tzs = [
            keep.tile([P, E], F32, name=f"tz{h}", tag=tag, align_bytes=64) for h, tag in enumerate(("xs_then_tz", "xw_then_tz"))
        ]
        for h in range(2):
            nc.sync.dma_start(tzs[h][:], tz[h * P : (h + 1) * P, :])
        b_ps = [psum.tile([P, 2, J], F32, name=f"b_ps{u}") for u in range(2)]
        for t in range(PACK):
            first_stage(b_ps[t // 2][:, t % 2, :], t, xb_w, xb_s)

        a_sb = [keep.tile([P, J], F32, name=f"a_sb{t}", align_bytes=64) for t in range(PACK)]
        picked = [keep.tile([P, J], F32, name=f"picked{t}", align_bytes=64) for t in range(PACK)]
        diff = keep.tile([P, PACK, J], F32, name="diff", tag="diff_then_gate", align_bytes=64)

        def pick_on_scalar(t):
            nc.scalar.activation(picked[t][:], boards[t][:].indirect(read[:]), ACT.Copy)

        def subtract(t):
            nc.vector.tensor_tensor(diff[:, t, :], picked[t][:], b_ps[t // 2][:, t % 2, :], ALU.subtract)

        nc.scalar.copy(a_sb[0][:], a_ps[0][:])
        nc.scalar.activation(boards[0][:].indirect(put[:]), a_sb[0][:], ACT.Copy)
        for t in (2, 3):
            nc.vector.tensor_copy(a_sb[t][:], a_ps[t][:])
            nc.vector.tensor_copy(boards[t][:].indirect(put[:]), a_sb[t][:])
        nc.scalar.copy(a_sb[1][:], a_ps[1][:])
        pick_on_scalar(0)
        nc.scalar.activation(boards[1][:].indirect(put[:]), a_sb[1][:], ACT.Copy)
        pick_on_scalar(2)
        pick_on_scalar(1)
        subtract(0)
        nc.vector.tensor_copy(picked[3][:], boards[3][:].indirect(read[:]))
        for t in (2, 3, 1):
            subtract(t)

        hid = keep.tile([P, J, PACK], BF16, align_bytes=64)
        half = 160
        woven = diff[:].rearrange("p t j -> p j t")
        nc.scalar.activation(
            hid[:, :half, :].rearrange("p (c i) t -> p c t i", i=4),
            diff[:, :, :half].rearrange("p t (c i) -> p c t i", i=4),
            ACT.Abs,
        )
        nc.vector.scalar_tensor_tensor(hid[:, half:, :], woven[:, half:, :], -1.0, woven[:, half:, :], ALU.mult, ALU.max)

        codes = keep.tile([P, J], U32, align_bytes=64)
        scales = keep.tile([P, J], U8, align_bytes=64)
        nc.vector.quantize_mx(out=codes[:].bitcast(E5M2X4), scales=scales[:], in_=hid[:].rearrange("p j t -> p (j t)"))

        gate = keep.tile([P, PACK, J], F32, name="gate", tag="diff_then_gate", align_bytes=64)
        res = [keep.tile([P, J], F32, name=f"res{h}", align_bytes=64) for h in range(2)]
        for h in range(2):
            nc.scalar.activation(
                gate[:, h, :], tzs[h][:].indirect(entry[:]), ACT.Sigmoid, bias=offset[:, h : h + 1], scale=slope[:, h : h + 1]
            )
            p_ps = psum.tile([P, J], F32, name=f"p_ps{h}")
            nc.tensor.matmul_mx(
                out=p_ps[:],
                lhsT=wbw[:, 2 * P * h : 2 * P * (h + 1)].bitcast(E2M1X4),
                lhsT_scale=wbs[:, P * h : P * (h + 1)],
                rhs=codes[:].bitcast(E5M2X4),
                rhs_scale=scales[:],
                start=True,
                stop=True,
            )
            nc.vector.tensor_tensor(res[h][:], gate[:, h, :], p_ps[:], ALU.mult)
            (nc.sync if h == 0 else nc.scalar).dma_start(out[h * P : (h + 1) * P, :], res[h][:])
